import numpy as np
import ml_dtypes

BF16 = ml_dtypes.bfloat16


def bf(x):
    return np.asarray(x, np.float32).astype(BF16)


def f32(x):
    return np.asarray(x, np.float32)


def f64(x):
    return np.asarray(x).astype(np.float64)


def striped(idx):
    return np.concatenate([l.reshape(-1, 16).T for l in idx])


def rows(idx, k):
    return np.tile(np.repeat(idx, 16, axis=0), (k // (16 * 8), 1))


def look(tab, idx):
    return np.take_along_axis(f64(tab), rows(idx, len(tab)), axis=1)


K, S, D, V, N = 256, 2048, 4, 512, 2048


def setup_inputs():
    return {"tab": f32(np.random.standard_normal((K, S))), "x0": f32(np.random.standard_normal((K, V))), "offs": striped(np.stack([np.random.permutation(S)[:N] for _ in range(8)]))}


def reference(tab, x0, offs):
    idx = np.stack([g.T.reshape(-1) for g in np.split(offs, 8)])
    x = f64(x0)
    for d in range(D):
        x = np.minimum(x, look(tab, idx[:, d * V:(d + 1) * V]))
    return x

@@ -1,0 +1,48 @@
+import concourse.mybir as mybir
+
+F32 = mybir.dt.float32
+U16 = mybir.dt.uint16
+MIN = mybir.AluOpType.min
+
+P = 128
+V = 512
+
+FLOPS = 256 * 512 * 4
+
+
+def tile_lookup_pool_min_out_kernel(tc, tab, x0, offs, out):
+    nc = tc.nc
+    rows, table_columns = tab.shape
+    blocks = rows // P
+    list_columns = offs.shape[1]
+    piece = V // 16
+    neighbours = list_columns // piece
+
+    tab_blocks = tab.rearrange("(b p) s -> b p s", p=P)
+    x0_blocks = x0.rearrange("(b p) v -> b p v", p=P)
+    out_blocks = out.rearrange("(b p) v -> b p v", p=P)
+
+    with (
+        tc.tile_pool(name="held", bufs=1) as held,
+        tc.tile_pool(name="running", bufs=neighbours) as running,
+    ):
+        offsets = held.tile([P, list_columns], U16, name="offsets")
+        nc.sync.dma_start(offsets[:], offs)
+
+        windows, centres = [], []
+        for b in range(blocks):
+            centre = held.tile([P, V], F32, name=f"centre{b}")
+            nc.sync.dma_start(centre[:], x0_blocks[b])
+            window = held.tile([P, table_columns], F32, name=f"window{b}")
+            nc.sync.dma_start(window[:], tab_blocks[b])
+            centres.append(centre)
+            windows.append(window)
+
+        for b in range(blocks):
+            smallest = centres[b]
+            for d in range(neighbours):
+                looked_up = windows[b][:].indirect(offsets[:, d * piece : (d + 1) * piece])
+                lower = running.tile([P, V], F32, name=f"lower{b}")
+                nc.vector.tensor_tensor(lower[:], looked_up, smallest[:], MIN)
+                smallest = lower
+            nc.sync.dma_start(out_blocks[b], smallest[:])

@@ -7,8 +7,6 @@ MIN = mybir.AluOpType.min
 P = 128
 V = 512
 
-FLOPS = 256 * 512 * 4
-
 
 def tile_lookup_pool_min_out_kernel(tc, tab, x0, offs, out):
     nc = tc.nc
@@ -24,7 +22,7 @@ def tile_lookup_pool_min_out_kernel(tc, tab, x0, offs, out):
 
     with (
         tc.tile_pool(name="held", bufs=1) as held,
-        tc.tile_pool(name="running", bufs=neighbours) as running,
+        tc.tile_pool(name="running", bufs=3) as running,
     ):
         offsets = held.tile([P, list_columns], U16, name="offsets")
         nc.sync.dma_start(offsets[:], offs)
@@ -38,11 +36,12 @@ def tile_lookup_pool_min_out_kernel(tc, tab, x0, offs, out):
             centres.append(centre)
             windows.append(window)
 
-        for b in range(blocks):
-            smallest = centres[b]
-            for d in range(neighbours):
+        smallest = [centre[:] for centre in centres]
+        for d in range(neighbours):
+            lower = running.tile([P, blocks, V], F32, name="lower")
+            for b in range(blocks):
                 looked_up = windows[b][:].indirect(offsets[:, d * piece : (d + 1) * piece])
-                lower = running.tile([P, V], F32, name=f"lower{b}")
-                nc.vector.tensor_tensor(lower[:], looked_up, smallest[:], MIN)
-                smallest = lower
-            nc.sync.dma_start(out_blocks[b], smallest[:])
+                nc.vector.tensor_tensor(lower[:, b], looked_up, smallest[b], MIN)
+                smallest[b] = lower[:, b]
+        for b in range(blocks):
+            nc.sync.dma_start(out_blocks[b], smallest[b])

import concourse.mybir as mybir

F32 = mybir.dt.float32
U16 = mybir.dt.uint16
MIN = mybir.AluOpType.min

P = 128
V = 512


def tile_lookup_pool_min_out_kernel(tc, tab, x0, offs, out):
    nc = tc.nc
    rows, table_columns = tab.shape
    blocks = rows // P
    list_columns = offs.shape[1]
    piece = V // 16
    neighbours = list_columns // piece

    tab_blocks = tab.rearrange("(b p) s -> b p s", p=P)
    x0_blocks = x0.rearrange("(b p) v -> b p v", p=P)
    out_blocks = out.rearrange("(b p) v -> b p v", p=P)

    with (
        tc.tile_pool(name="held", bufs=1) as held,
        tc.tile_pool(name="running", bufs=3) as running,
    ):
        offsets = held.tile([P, list_columns], U16, name="offsets")
        nc.sync.dma_start(offsets[:], offs)

        windows, centres = [], []
        for b in range(blocks):
            centre = held.tile([P, V], F32, name=f"centre{b}")
            nc.sync.dma_start(centre[:], x0_blocks[b])
            window = held.tile([P, table_columns], F32, name=f"window{b}")
            nc.sync.dma_start(window[:], tab_blocks[b])
            centres.append(centre)
            windows.append(window)

        smallest = [centre[:] for centre in centres]
        for d in range(neighbours):
            lower = running.tile([P, blocks, V], F32, name="lower")
            for b in range(blocks):
                looked_up = windows[b][:].indirect(offsets[:, d * piece : (d + 1) * piece])
                nc.vector.tensor_tensor(lower[:, b], looked_up, smallest[b], MIN)
                smallest[b] = lower[:, b]
        for b in range(blocks):
            nc.sync.dma_start(out_blocks[b], smallest[b])
